import numpy as np
import ml_dtypes


def mxq(x, axis, fmt="e4m3"):
    dtype, down = {"e4m3": (ml_dtypes.float8_e4m3fn, 7), "e5m2": (ml_dtypes.float8_e5m2, 14)}[fmt]
    v = np.moveaxis(np.asarray(x, np.float32).astype(ml_dtypes.bfloat16).astype(np.float64), axis, -1)
    blocks = v.reshape(v.shape[:-1] + (-1, 32))
    amax = np.abs(blocks).max(-1, keepdims=True)
    byte = np.maximum(np.where(amax > 0, np.frexp(amax)[1] - 1 + 127, 0) - down, 1)
    scale = np.exp2(byte - 127.0)
    codes = (blocks / scale).astype(np.float32).astype(dtype).astype(np.float64)
    return np.moveaxis((codes * scale).reshape(v.shape), -1, axis)


WIDE = False


def mx_kscale(k):
    if not WIDE:
        return np.ones(k)
    levels = np.array([30, -30])
    if k % 512:
        return np.exp2(np.random.permutation(np.resize(levels, k // 32))).repeat(32)
    a = np.empty((k // 512, 16))
    for p in range(k // 512):
        a[p, :8] = np.random.permutation(np.resize(levels, 8))
        for g in range(8):
            far = levels[np.abs(levels - a[p, g]) >= 10]
            a[p, g + 8] = far[np.random.randint(len(far))]
    return np.exp2(a.ravel()).repeat(32)


BF16 = ml_dtypes.bfloat16


def bf(x):
    return np.asarray(x, np.float32).astype(BF16)


def f64(x):
    return np.asarray(x).astype(np.float64)


E2M1 = np.array([0.0, 0.5, 1.0, 1.5, 2.0, 3.0, 4.0, 6.0, -0.0, -0.5, -1.0, -1.5, -2.0, -3.0, -4.0, -6.0])


def pack_weight(w, fmt):
    k, n = w.shape
    w = f64(bf(w)).reshape(k // 32, 32, n)
    amax = np.abs(w).max(1)
    if fmt in ("e4m3", "e5m2"):
        byte = np.frexp(amax)[1] - 1 + 127 - (7 if fmt == "e4m3" else 14)
    else:
        mant, ex = np.frexp(amax / 6.0)
        byte = np.where(mant > 0.5, ex, ex - 1) + 127
    byte = np.clip(np.where(amax > 0, byte, 1), 1, 254)
    scaled = (w * np.exp2(127.0 - byte)[:, None, :]).reshape(k, n).astype(np.float32)
    by_word = np.ascontiguousarray(scaled.reshape(k // 512, 128, 4, n).transpose(0, 1, 3, 2))
    if fmt in ("e4m3", "e5m2"):
        words = by_word.astype(ml_dtypes.float8_e4m3fn if fmt == "e4m3" else ml_dtypes.float8_e5m2).view(np.uint8)
    else:
        c = by_word.astype(ml_dtypes.float4_e2m1fn).view(np.uint8) & 0xF
        words = c[..., 0::2] | (c[..., 1::2] << 4)
    return np.ascontiguousarray(words), np.ascontiguousarray(byte.astype(np.uint8).reshape(k // 512, 16, n))


def unpack_weight(words, scales, fmt):
    g, p, n, _ = words.shape
    if fmt in ("e4m3", "e5m2"):
        vals = np.ascontiguousarray(words).view(ml_dtypes.float8_e4m3fn if fmt == "e4m3" else ml_dtypes.float8_e5m2).astype(np.float64)
    else:
        nib = np.empty((g, p, n, 4), np.uint8)
        nib[..., 0::2] = words & 0xF
        nib[..., 1::2] = words >> 4
        vals = E2M1[nib]
    vals = vals * np.repeat(np.exp2(scales.astype(np.float64) - 127.0), 8, axis=1)[..., None]
    return vals.transpose(0, 1, 3, 2).reshape(g * 512, n)


R, T, H, S, D = 4, 1024, 4, 1024, 128
C = R * T


def setup_inputs():
    s = mx_kscale(C)
    a = np.exp(np.random.standard_normal((C, H, S)))
    a = a / a.sum(axis=2, keepdims=True)
    da = np.random.standard_normal((C, H, S)) * S * np.sqrt(D / C)
    G = a * (da - (a * da).sum(axis=2, keepdims=True)) * s[:, None, None]
    G_words, G_scales = pack_weight(G.reshape(C, H * S), "e5m2")
    return {"g_words": G_words,
            "g_scales": G_scales,
            "queries": bf(np.random.standard_normal((C, H * D)) / s[:, None]),
            "gain": bf(1 + 0.1 * np.random.standard_normal((H, D))),
            "acc": bf(np.random.standard_normal((H, S, D)))}


def reference(g_words, g_scales, queries, gain, acc):
    G = unpack_weight(g_words, g_scales, "e5m2")
    x = mxq(f64(queries), 0, "e4m3")
    y = G.reshape(C, H, S).transpose(1, 2, 0) @ x.reshape(C, H, D).transpose(1, 0, 2)
    dk = y * f64(gain)[:, None, :] / np.sqrt(D)
    return f64(acc) + dk

@@ -1,0 +1,230 @@
+import math
+from contextlib import ExitStack
+
+import concourse.mybir as mybir
+from concourse.masks import make_identity
+
+F32 = mybir.dt.float32
+BF16 = mybir.dt.bfloat16
+U32 = mybir.dt.uint32
+I32 = mybir.dt.int32
+U8 = mybir.dt.uint8
+E4X4 = mybir.dt.float8_e4m3fn_x4
+E5X4 = mybir.dt.float8_e5m2_x4
+COPY = mybir.ActivationFunctionType.Copy
+MULT = mybir.AluOpType.mult
+ADD = mybir.AluOpType.add
+
+P = 128
+HEADS = 4
+KEYS = 1024
+D = 128
+K = 4096
+GROUPS = K // 512
+W = HEADS * D
+N = 512
+WHOLE = 6
+FLOPS = 2 * K * HEADS * KEYS * D
+
+
+def tile_grouped_key_gradient_e2_kernel(tc, g_words, g_scales, queries, gain, acc, out):
+    nc = tc.nc
+    with ExitStack() as ctx:
+        keep = ctx.enter_context(tc.tile_pool(name="keep", bufs=1))
+        qpool = ctx.enter_context(tc.tile_pool(name="qpool", bufs=4))
+        mixpool = ctx.enter_context(tc.tile_pool(name="mixpool", bufs=3))
+        gpool = ctx.enter_context(tc.tile_pool(name="gpool", bufs=4))
+        ypool = ctx.enter_context(tc.tile_pool(name="ypool", bufs=2))
+        psum = ctx.enter_context(tc.psum_pool(name="psum", bufs=1))
+        ctx.enter_context(tc.manual_schedule())
+
+        ident = keep.tile([P, P], F32, name="ident", align_bytes=64)
+        gain_rows = keep.tile([P, P], BF16, name="gain_rows", align_bytes=64)
+        gain_f32 = keep.tile([P, P], F32, name="gain_f32", align_bytes=64)
+        gain_col = keep.tile([P, HEADS], F32, name="gain_col", align_bytes=64)
+        gsc = keep.tile([P, GROUPS * HEADS * KEYS], U8, name="gsc", align_bytes=64)
+        xc = keep.tile([P, GROUPS, W], U32, name="xc", align_bytes=64)
+        xs = keep.tile([P, GROUPS, W], U8, name="xs", align_bytes=64)
+        acc_a = keep.tile([P, HEADS - 1, KEYS], BF16, name="acc_a", align_bytes=64)
+        acc_b = keep.tile([P, 2, N], BF16, name="acc_b", align_bytes=64)
+
+        nc.vector.memset(gain_rows[:], 0.0)
+        nc.scalar.dma_start(out=gain_rows[0:HEADS, :], in_=gain)
+        make_identity(nc, ident[:])
+
+        raws = []
+        for i in range(4):
+            raw = qpool.tile([P, 2, 4 * W], BF16, name="raw", tag="raw", align_bytes=64)
+            nc.sync.dma_start(
+                out=raw[:],
+                in_=queries[1024 * i : 1024 * (i + 1), :].rearrange("(g p j) w -> p g (j w)", g=2, j=4),
+            )
+            raws.append(raw)
+        nc.vector.memset(gsc[:].bitcast(I32), 0)
+        scale_rows = g_scales.rearrange("g (q r) n -> r q g n", r=4)
+        for r in range(4):
+            nc.sync.dma_start(
+                out=gsc[r:P:32, :].bitcast(I32).rearrange("q (g n) -> q g n", g=GROUPS),
+                in_=scale_rows[r].bitcast(I32),
+            )
+
+        def load_group(g):
+            t = gpool.tile([P, HEADS * KEYS], U32, name="gw", tag="gw", align_bytes=64)
+            nc.sync.dma_start(
+                out=t[:].bitcast(I32),
+                in_=g_words[g].rearrange("p n t -> p (n t)").bitcast(I32),
+            )
+            return t
+
+        def load_tail(g0, g1, n0, n1, name):
+            t = keep.tile([P, g1 - g0, n1 - n0], U32, name=name, align_bytes=64)
+            nc.sync.dma_start(
+                out=t[:].bitcast(I32),
+                in_=g_words[g0:g1, :, n0:n1, :].rearrange("g p n t -> p g (n t)").bitcast(I32),
+            )
+            return t
+
+        words = {}
+        for g in range(4):
+            words[g] = load_group(g)
+        nc.sync.dma_start(out=acc_a[:], in_=acc[0:3].rearrange("h (p j) d -> p h (j d)", p=P))
+        nc.sync.dma_start(out=acc_b[:], in_=acc[3].rearrange("(u p j) d -> p u (j d)", u=2, p=P))
+
+        nc.vector.tensor_copy(out=gain_f32[:], in_=gain_rows[:])
+        gps = psum.tile([P, P], F32, name="gps", tag="b7")
+        nc.tensor.transpose(gps[:], gain_f32[:], ident[:])
+
+        mixes = {}
+
+        def interleave(g):
+            mix = mixpool.tile([P, W, 4], BF16, name="mix", tag="mix", align_bytes=64)
+            nc.vector.tensor_copy(
+                out=mix[:], in_=raws[g // 2][:, g % 2, :].rearrange("p (j w) -> p w j", j=4)
+            )
+            mixes[g] = mix
+
+        def quantise(g):
+            nc.vector.quantize_mx(
+                out=xc[:, g, :].bitcast(E4X4),
+                scales=xs[:, g, :],
+                in_=mixes[g][:].rearrange("p w j -> p (w j)"),
+            )
+
+        interleave(0)
+        nc.vector.tensor_scalar(
+            out=gain_col[:], in0=gps[:, 0:HEADS], scalar1=1.0 / math.sqrt(D), scalar2=None, op0=MULT
+        )
+        for g in range(1, GROUPS):
+            interleave(g)
+            quantise(g - 1)
+        quantise(GROUPS - 1)
+
+        banks = {}
+        for h in range(HEADS):
+            for u in range(2):
+                banks[(h, u)] = psum.tile([P, N], F32, name="y%d%d" % (h, u), tag="b%d" % (2 * h + u))
+
+        def mm(h, u, g, w):
+            n0 = KEYS * h + N * u
+            nc.tensor.matmul_mx(
+                out=banks[(h, u)][:],
+                lhsT=xc[:, g, D * h : D * (h + 1)].bitcast(E4X4),
+                lhsT_scale=xs[:, g, D * h : D * (h + 1)],
+                rhs=w.bitcast(E5X4),
+                rhs_scale=gsc[:, HEADS * KEYS * g + n0 : HEADS * KEYS * g + n0 + N],
+                start=(g == 0),
+                stop=(g == GROUPS - 1),
+            )
+
+        for g in range(WHOLE):
+            for h in range(HEADS):
+                for u in range(2):
+                    n0 = KEYS * h + N * u
+                    mm(h, u, g, words[g][:, n0 : n0 + N])
+            if g + 4 < WHOLE:
+                words[g + 4] = load_group(g + 4)
+            if g + 5 == WHOLE:
+                tails = [load_tail(WHOLE, GROUPS, KEYS * h, KEYS * (h + 1), "gt%d" % h) for h in range(3)]
+                t3 = load_tail(6, 7, 3 * KEYS, 4 * KEYS, "gt3")
+                t3u = [
+                    load_tail(7, 8, 3 * KEYS + N * u, 3 * KEYS + N * (u + 1), "gt3u%d" % u) for u in range(2)
+                ]
+
+        def mm_tail(h):
+            for g in range(WHOLE, GROUPS):
+                for u in range(2):
+                    mm(h, u, g, tails[h][:, g - WHOLE, N * u : N * (u + 1)])
+
+        def head_out(h):
+            y = ypool.tile([P, 8, P], F32, name="y", tag="y", align_bytes=64)
+            nc.scalar.activation(
+                out=y[:, :, 0:64],
+                in_=banks[(h, 0)][:].rearrange("d (p j) -> d j p", j=8),
+                func=COPY,
+                scale=gain_col[:, h : h + 1],
+            )
+            nc.vector.tensor_scalar(
+                out=y[:, :, 64:128],
+                in0=banks[(h, 1)][:].rearrange("d (p j) -> d j p", j=8),
+                scalar1=gain_col[:, h : h + 1],
+                scalar2=None,
+                op0=MULT,
+            )
+            o = keep.tile([P, KEYS], F32, name="o%d" % h, align_bytes=64)
+            ts = []
+            for half in range(2):
+                t = psum.tile([P, 4, D], F32, name="t%d%d" % (h, half), tag="b%d" % (2 * h + half))
+                for j in range(4):
+                    nc.tensor.transpose(t[:, j, :], y[:, 4 * half + j, :], ident[:])
+                ts.append(t)
+            for half in range(2):
+                cols = slice(N * half, N * (half + 1))
+                nc.vector.tensor_tensor(
+                    out=o[:, cols],
+                    in0=ts[half][:].rearrange("p j d -> p (j d)"),
+                    in1=acc_a[:, h, cols],
+                    op=ADD,
+                )
+            nc.sync.dma_start(out=out[h].rearrange("(p j) d -> p (j d)", p=P), in_=o[:])
+
+        mm_tail(0)
+        mm_tail(1)
+        head_out(0)
+        mm_tail(2)
+        head_out(1)
+        for u in range(2):
+            mm(3, u, 6, t3[:, 0, N * u : N * (u + 1)])
+        mm(3, 0, 7, t3u[0][:, 0, :])
+        head_out(2)
+        mm(3, 1, 7, t3u[1][:, 0, :])
+
+        o3 = [keep.tile([P, N], F32, name="o3%d" % u, align_bytes=64) for u in range(2)]
+        y3 = [keep.tile([P, 4, P], F32, name="y3%d" % u, align_bytes=64) for u in range(2)]
+        t3s = {}
+        for u in range(2):
+            for half in range(2):
+                jj = slice(2 * half, 2 * half + 2)
+                nc.scalar.activation(
+                    out=y3[u][:, jj, :],
+                    in_=banks[(3, u)][:].rearrange("d (p j) -> d j p", j=4)[:, jj, :],
+                    func=COPY,
+                    scale=gain_col[:, 3:4],
+                )
+        for u in range(2):
+            for half in range(2):
+                t = psum.tile([P, 2, D], F32, name="t3%d%d" % (u, half), tag="b%d" % (2 * u + half))
+                for j in range(2):
+                    nc.tensor.transpose(t[:, j, :], y3[u][:, 2 * half + j, :], ident[:])
+                t3s[(u, half)] = t
+        for u in range(2):
+            dst = out[3, N * u : N * (u + 1)].rearrange("(p j) d -> p (j d)", p=P)
+            for half in range(2):
+                cols = slice(256 * half, 256 * (half + 1))
+                nc.vector.tensor_tensor(
+                    out=o3[u][:, cols],
+                    in0=t3s[(u, half)][:].rearrange("p j d -> p (j d)"),
+                    in1=acc_b[:, u, cols],
+                    op=ADD,
+                )
+                queue = nc.sync if half == 0 else nc.scalar
+                queue.dma_start(out=dst[:, cols], in_=o3[u][:, cols])

@@ -31,7 +31,6 @@ def tile_grouped_key_gradient_e2_kernel(tc, g_words, g_scales, queries, gain, ac
     nc = tc.nc
     with ExitStack() as ctx:
         keep = ctx.enter_context(tc.tile_pool(name="keep", bufs=1))
-        qpool = ctx.enter_context(tc.tile_pool(name="qpool", bufs=4))
         mixpool = ctx.enter_context(tc.tile_pool(name="mixpool", bufs=3))
         gpool = ctx.enter_context(tc.tile_pool(name="gpool", bufs=4))
         ypool = ctx.enter_context(tc.tile_pool(name="ypool", bufs=2))
@@ -52,21 +51,31 @@ def tile_grouped_key_gradient_e2_kernel(tc, g_words, g_scales, queries, gain, ac
         nc.scalar.dma_start(out=gain_rows[0:HEADS, :], in_=gain)
         make_identity(nc, ident[:])
 
-        raws = []
-        for i in range(4):
-            raw = qpool.tile([P, 2, 4 * W], BF16, name="raw", tag="raw", align_bytes=64)
+        raws = {}
+
+        def load_queries(g0, g1):
+            raw = keep.tile([P, g1 - g0, 4 * W], BF16, name="raw%d" % g0, align_bytes=64)
             nc.sync.dma_start(
                 out=raw[:],
-                in_=queries[1024 * i : 1024 * (i + 1), :].rearrange("(g p j) w -> p g (j w)", g=2, j=4),
+                in_=queries[512 * g0 : 512 * g1, :].rearrange("(g p j) w -> p g (j w)", p=P, j=4),
             )
-            raws.append(raw)
-        nc.vector.memset(gsc[:].bitcast(I32), 0)
+            for g in range(g0, g1):
+                raws[g] = raw[:, g - g0, :]
+
+        load_queries(0, 1)
+        row = HEADS * KEYS
         scale_rows = g_scales.rearrange("g (q r) n -> r q g n", r=4)
-        for r in range(4):
-            nc.sync.dma_start(
-                out=gsc[r:P:32, :].bitcast(I32).rearrange("q (g n) -> q g n", g=GROUPS),
-                in_=scale_rows[r].bitcast(I32),
-            )
+        for g in range(0, GROUPS, 2):
+            nc.vector.memset(gsc[:, row * g : row * (g + 2)].bitcast(I32), 0)
+        for g0, g1 in ((0, 2), (2, 4), (4, 6), (6, 7), (7, 8)):
+            for r in range(4):
+                nc.sync.dma_start(
+                    out=gsc[r:P:32, row * g0 : row * g1].bitcast(I32).rearrange("q (g n) -> q g n", g=g1 - g0),
+                    in_=scale_rows[r, :, g0:g1, :].bitcast(I32),
+                )
+        load_queries(1, 2)
+        for g in range(2, GROUPS, 2):
+            load_queries(g, g + 2)
 
         def load_group(g):
             t = gpool.tile([P, HEADS * KEYS], U32, name="gw", tag="gw", align_bytes=64)
@@ -99,7 +108,7 @@ def tile_grouped_key_gradient_e2_kernel(tc, g_words, g_scales, queries, gain, ac
         def interleave(g):
             mix = mixpool.tile([P, W, 4], BF16, name="mix", tag="mix", align_bytes=64)
             nc.vector.tensor_copy(
-                out=mix[:], in_=raws[g // 2][:, g % 2, :].rearrange("p (j w) -> p w j", j=4)
+                out=mix[:], in_=raws[g].rearrange("p (j w) -> p w j", j=4)
             )
             mixes[g] = mix
 

import math
from contextlib import ExitStack

import concourse.mybir as mybir
from concourse.masks import make_identity

F32 = mybir.dt.float32
BF16 = mybir.dt.bfloat16
U32 = mybir.dt.uint32
I32 = mybir.dt.int32
U8 = mybir.dt.uint8
E4X4 = mybir.dt.float8_e4m3fn_x4
E5X4 = mybir.dt.float8_e5m2_x4
COPY = mybir.ActivationFunctionType.Copy
MULT = mybir.AluOpType.mult
ADD = mybir.AluOpType.add

P = 128
HEADS = 4
KEYS = 1024
D = 128
K = 4096
GROUPS = K // 512
W = HEADS * D
N = 512
WHOLE = 6
FLOPS = 2 * K * HEADS * KEYS * D


def tile_grouped_key_gradient_e2_kernel(tc, g_words, g_scales, queries, gain, acc, out):
    nc = tc.nc
    with ExitStack() as ctx:
        keep = ctx.enter_context(tc.tile_pool(name="keep", bufs=1))
        mixpool = ctx.enter_context(tc.tile_pool(name="mixpool", bufs=3))
        gpool = ctx.enter_context(tc.tile_pool(name="gpool", bufs=4))
        ypool = ctx.enter_context(tc.tile_pool(name="ypool", bufs=2))
        psum = ctx.enter_context(tc.psum_pool(name="psum", bufs=1))
        ctx.enter_context(tc.manual_schedule())

        ident = keep.tile([P, P], F32, name="ident", align_bytes=64)
        gain_rows = keep.tile([P, P], BF16, name="gain_rows", align_bytes=64)
        gain_f32 = keep.tile([P, P], F32, name="gain_f32", align_bytes=64)
        gain_col = keep.tile([P, HEADS], F32, name="gain_col", align_bytes=64)
        gsc = keep.tile([P, GROUPS * HEADS * KEYS], U8, name="gsc", align_bytes=64)
        xc = keep.tile([P, GROUPS, W], U32, name="xc", align_bytes=64)
        xs = keep.tile([P, GROUPS, W], U8, name="xs", align_bytes=64)
        acc_a = keep.tile([P, HEADS - 1, KEYS], BF16, name="acc_a", align_bytes=64)
        acc_b = keep.tile([P, 2, N], BF16, name="acc_b", align_bytes=64)

        nc.vector.memset(gain_rows[:], 0.0)
        nc.scalar.dma_start(out=gain_rows[0:HEADS, :], in_=gain)
        make_identity(nc, ident[:])

        raws = {}

        def load_queries(g0, g1):
            raw = keep.tile([P, g1 - g0, 4 * W], BF16, name="raw%d" % g0, align_bytes=64)
            nc.sync.dma_start(
                out=raw[:],
                in_=queries[512 * g0 : 512 * g1, :].rearrange("(g p j) w -> p g (j w)", p=P, j=4),
            )
            for g in range(g0, g1):
                raws[g] = raw[:, g - g0, :]

        load_queries(0, 1)
        row = HEADS * KEYS
        scale_rows = g_scales.rearrange("g (q r) n -> r q g n", r=4)
        for g in range(0, GROUPS, 2):
            nc.vector.memset(gsc[:, row * g : row * (g + 2)].bitcast(I32), 0)
        for g0, g1 in ((0, 2), (2, 4), (4, 6), (6, 7), (7, 8)):
            for r in range(4):
                nc.sync.dma_start(
                    out=gsc[r:P:32, row * g0 : row * g1].bitcast(I32).rearrange("q (g n) -> q g n", g=g1 - g0),
                    in_=scale_rows[r, :, g0:g1, :].bitcast(I32),
                )
        load_queries(1, 2)
        for g in range(2, GROUPS, 2):
            load_queries(g, g + 2)

        def load_group(g):
            t = gpool.tile([P, HEADS * KEYS], U32, name="gw", tag="gw", align_bytes=64)
            nc.sync.dma_start(
                out=t[:].bitcast(I32),
                in_=g_words[g].rearrange("p n t -> p (n t)").bitcast(I32),
            )
            return t

        def load_tail(g0, g1, n0, n1, name):
            t = keep.tile([P, g1 - g0, n1 - n0], U32, name=name, align_bytes=64)
            nc.sync.dma_start(
                out=t[:].bitcast(I32),
                in_=g_words[g0:g1, :, n0:n1, :].rearrange("g p n t -> p g (n t)").bitcast(I32),
            )
            return t

        words = {}
        for g in range(4):
            words[g] = load_group(g)
        nc.sync.dma_start(out=acc_a[:], in_=acc[0:3].rearrange("h (p j) d -> p h (j d)", p=P))
        nc.sync.dma_start(out=acc_b[:], in_=acc[3].rearrange("(u p j) d -> p u (j d)", u=2, p=P))

        nc.vector.tensor_copy(out=gain_f32[:], in_=gain_rows[:])
        gps = psum.tile([P, P], F32, name="gps", tag="b7")
        nc.tensor.transpose(gps[:], gain_f32[:], ident[:])

        mixes = {}

        def interleave(g):
            mix = mixpool.tile([P, W, 4], BF16, name="mix", tag="mix", align_bytes=64)
            nc.vector.tensor_copy(
                out=mix[:], in_=raws[g].rearrange("p (j w) -> p w j", j=4)
            )
            mixes[g] = mix

        def quantise(g):
            nc.vector.quantize_mx(
                out=xc[:, g, :].bitcast(E4X4),
                scales=xs[:, g, :],
                in_=mixes[g][:].rearrange("p w j -> p (w j)"),
            )

        interleave(0)
        nc.vector.tensor_scalar(
            out=gain_col[:], in0=gps[:, 0:HEADS], scalar1=1.0 / math.sqrt(D), scalar2=None, op0=MULT
        )
        for g in range(1, GROUPS):
            interleave(g)
            quantise(g - 1)
        quantise(GROUPS - 1)

        banks = {}
        for h in range(HEADS):
            for u in range(2):
                banks[(h, u)] = psum.tile([P, N], F32, name="y%d%d" % (h, u), tag="b%d" % (2 * h + u))

        def mm(h, u, g, w):
            n0 = KEYS * h + N * u
            nc.tensor.matmul_mx(
                out=banks[(h, u)][:],
                lhsT=xc[:, g, D * h : D * (h + 1)].bitcast(E4X4),
                lhsT_scale=xs[:, g, D * h : D * (h + 1)],
                rhs=w.bitcast(E5X4),
                rhs_scale=gsc[:, HEADS * KEYS * g + n0 : HEADS * KEYS * g + n0 + N],
                start=(g == 0),
                stop=(g == GROUPS - 1),
            )

        for g in range(WHOLE):
            for h in range(HEADS):
                for u in range(2):
                    n0 = KEYS * h + N * u
                    mm(h, u, g, words[g][:, n0 : n0 + N])
            if g + 4 < WHOLE:
                words[g + 4] = load_group(g + 4)
            if g + 5 == WHOLE:
                tails = [load_tail(WHOLE, GROUPS, KEYS * h, KEYS * (h + 1), "gt%d" % h) for h in range(3)]
                t3 = load_tail(6, 7, 3 * KEYS, 4 * KEYS, "gt3")
                t3u = [
                    load_tail(7, 8, 3 * KEYS + N * u, 3 * KEYS + N * (u + 1), "gt3u%d" % u) for u in range(2)
                ]

        def mm_tail(h):
            for g in range(WHOLE, GROUPS):
                for u in range(2):
                    mm(h, u, g, tails[h][:, g - WHOLE, N * u : N * (u + 1)])

        def head_out(h):
            y = ypool.tile([P, 8, P], F32, name="y", tag="y", align_bytes=64)
            nc.scalar.activation(
                out=y[:, :, 0:64],
                in_=banks[(h, 0)][:].rearrange("d (p j) -> d j p", j=8),
                func=COPY,
                scale=gain_col[:, h : h + 1],
            )
            nc.vector.tensor_scalar(
                out=y[:, :, 64:128],
                in0=banks[(h, 1)][:].rearrange("d (p j) -> d j p", j=8),
                scalar1=gain_col[:, h : h + 1],
                scalar2=None,
                op0=MULT,
            )
            o = keep.tile([P, KEYS], F32, name="o%d" % h, align_bytes=64)
            ts = []
            for half in range(2):
                t = psum.tile([P, 4, D], F32, name="t%d%d" % (h, half), tag="b%d" % (2 * h + half))
                for j in range(4):
                    nc.tensor.transpose(t[:, j, :], y[:, 4 * half + j, :], ident[:])
                ts.append(t)
            for half in range(2):
                cols = slice(N * half, N * (half + 1))
                nc.vector.tensor_tensor(
                    out=o[:, cols],
                    in0=ts[half][:].rearrange("p j d -> p (j d)"),
                    in1=acc_a[:, h, cols],
                    op=ADD,
                )
            nc.sync.dma_start(out=out[h].rearrange("(p j) d -> p (j d)", p=P), in_=o[:])

        mm_tail(0)
        mm_tail(1)
        head_out(0)
        mm_tail(2)
        head_out(1)
        for u in range(2):
            mm(3, u, 6, t3[:, 0, N * u : N * (u + 1)])
        mm(3, 0, 7, t3u[0][:, 0, :])
        head_out(2)
        mm(3, 1, 7, t3u[1][:, 0, :])

        o3 = [keep.tile([P, N], F32, name="o3%d" % u, align_bytes=64) for u in range(2)]
        y3 = [keep.tile([P, 4, P], F32, name="y3%d" % u, align_bytes=64) for u in range(2)]
        t3s = {}
        for u in range(2):
            for half in range(2):
                jj = slice(2 * half, 2 * half + 2)
                nc.scalar.activation(
                    out=y3[u][:, jj, :],
                    in_=banks[(3, u)][:].rearrange("d (p j) -> d j p", j=4)[:, jj, :],
                    func=COPY,
                    scale=gain_col[:, 3:4],
                )
        for u in range(2):
            for half in range(2):
                t = psum.tile([P, 2, D], F32, name="t3%d%d" % (u, half), tag="b%d" % (2 * u + half))
                for j in range(2):
                    nc.tensor.transpose(t[:, j, :], y3[u][:, 2 * half + j, :], ident[:])
                t3s[(u, half)] = t
        for u in range(2):
            dst = out[3, N * u : N * (u + 1)].rearrange("(p j) d -> p (j d)", p=P)
            for half in range(2):
                cols = slice(256 * half, 256 * (half + 1))
                nc.vector.tensor_tensor(
                    out=o3[u][:, cols],
                    in0=t3s[(u, half)][:].rearrange("p j d -> p (j d)"),
                    in1=acc_b[:, u, cols],
                    op=ADD,
                )
                queue = nc.sync if half == 0 else nc.scalar
                queue.dma_start(out=dst[:, cols], in_=o3[u][:, cols])
